import numpy as np
import ml_dtypes


def mxq(x, axis, fmt="e4m3"):
    dtype, down = {"e4m3": (ml_dtypes.float8_e4m3fn, 7), "e5m2": (ml_dtypes.float8_e5m2, 14)}[fmt]
    v = np.moveaxis(np.asarray(x, np.float32).astype(ml_dtypes.bfloat16).astype(np.float64), axis, -1)
    blocks = v.reshape(v.shape[:-1] + (-1, 32))
    amax = np.abs(blocks).max(-1, keepdims=True)
    byte = np.maximum(np.where(amax > 0, np.frexp(amax)[1] - 1 + 127, 0) - down, 1)
    scale = np.exp2(byte - 127.0)
    codes = (blocks / scale).astype(np.float32).astype(dtype).astype(np.float64)
    return np.moveaxis((codes * scale).reshape(v.shape), -1, axis)


WIDE = False


def mx_kscale(k):
    if not WIDE:
        return np.ones(k)
    levels = np.array([10, -10, 5, -5, 0])
    if k % 512:
        return np.exp2(np.random.permutation(np.resize(levels, k // 32))).repeat(32)
    a = np.empty((k // 512, 16))
    for p in range(k // 512):
        a[p, :8] = np.random.permutation(np.resize(levels, 8))
        for g in range(8):
            far = levels[np.abs(levels - a[p, g]) >= 10]
            a[p, g + 8] = far[np.random.randint(len(far))]
    return np.exp2(a.ravel()).repeat(32)


def f64(x):
    return np.asarray(x).astype(np.float64)


def striped8(idx):
    return np.asarray(idx).reshape(8, -1, 16).transpose(0, 2, 1).reshape(128, -1).astype(np.uint16)


def unstriped8(offs):
    return offs.reshape(8, 16, -1).transpose(0, 2, 1).reshape(8, -1).astype(np.int64)


def pick8(x, idx, run):
    r = np.arange(len(x))
    return x[r[:, None], idx[r % (8 * run) // run]]


E2M1 = np.array([0.0, 0.5, 1.0, 1.5, 2.0, 3.0, 4.0, 6.0, -0.0, -0.5, -1.0, -1.5, -2.0, -3.0, -4.0, -6.0])


def pack_weight(w, fmt):
    k, n = w.shape
    w = f64(np.asarray(w, np.float32).astype(ml_dtypes.bfloat16)).reshape(k // 32, 32, n)
    amax = np.abs(w).max(1)
    if fmt == "e4m3":
        byte = np.frexp(amax)[1] - 1 + 127 - 7
    else:
        mant, ex = np.frexp(amax / 6.0)
        byte = np.where(mant > 0.5, ex, ex - 1) + 127
    byte = np.clip(np.where(amax > 0, byte, 1), 1, 254)
    scaled = (w * np.exp2(127.0 - byte)[:, None, :]).reshape(k, n).astype(np.float32)
    by_word = np.ascontiguousarray(scaled.reshape(k // 512, 128, 4, n).transpose(0, 1, 3, 2))
    if fmt == "e4m3":
        words = by_word.astype(ml_dtypes.float8_e4m3fn).view(np.uint8)
    else:
        c = by_word.astype(ml_dtypes.float4_e2m1fn).view(np.uint8) & 0xF
        words = (c[..., 0::2] | (c[..., 1::2] << 4)).reshape(k // 512, 128, 2 * n)
    return np.ascontiguousarray(words), np.ascontiguousarray(byte.astype(np.uint8).reshape(k // 512, 16, n))


def unpack_weight(words, scales, fmt):
    g, _, n = scales.shape
    words = np.ascontiguousarray(words).reshape(g, 128, n, -1)
    if fmt == "e4m3":
        vals = words.view(ml_dtypes.float8_e4m3fn).astype(np.float64)
    else:
        nib = np.empty((g, 128, n, 4), np.uint8)
        nib[..., 0::2] = words & 0xF
        nib[..., 1::2] = words >> 4
        vals = E2M1[nib]
    vals = vals * np.repeat(np.exp2(scales.astype(np.float64) - 127.0), 8, axis=1)[..., None]
    return vals.transpose(0, 1, 3, 2).reshape(g * 512, n)


def sigmoid(v):
    return 1.0 / (1.0 + np.exp(-v))


D, T, I, Q = 512, 1024, 512, 128


def setup_inputs():
    n = np.random.standard_normal
    idx = np.stack([np.random.permutation(T)[:I] for _ in range(8)])
    idx2 = np.stack([np.random.permutation(T)[:I] for _ in range(8)])
    idx3 = np.stack([np.random.permutation(T)[:I] for _ in range(8)])
    idx4 = np.stack([np.random.permutation(T)[:I] for _ in range(8)])
    fd = mx_kscale(D)
    keysp = pack_weight(n((D, T)) / fd[:, None], "e4m3")
    tagsp = pack_weight(n((D, T)) / fd[:, None], "e2m1")
    return {
        "query": (n((D, Q)) * 0.75 / np.sqrt(D) * fd[:, None]).astype(np.float32),
        "query2": (n((D, Q)) * 0.75 / np.sqrt(D) * fd[:, None]).astype(np.float32),
        "keys_words": keysp[0],
        "keys_scales": keysp[1],
        "tags_words": tagsp[0],
        "tags_scales": tagsp[1],
        "thr": (np.random.uniform(-0.6, 0.6, (Q, 1))).astype(np.float32),
        "slope": (np.random.uniform(0.8, 2.0, (Q, 1))).astype(np.float32),
        "offs": striped8(idx),
        "offs2": striped8(idx2),
        "offs3": striped8(idx3),
        "offs4": striped8(idx4),
    }


def reference(query, query2, keys_words, keys_scales, tags_words, tags_scales, thr, slope, offs, offs2, offs3, offs4):
    idx = unstriped8(offs)
    idx2 = unstriped8(offs2)
    idx3 = unstriped8(offs3)
    idx4 = unstriped8(offs4)
    keysu = unpack_weight(keys_words, keys_scales, "e4m3")
    tagsu = unpack_weight(tags_words, tags_scales, "e2m1")
    queryq = mxq(f64(query), 0, "e4m3")
    query2q = mxq(f64(query2), 0, "e4m3")
    a = queryq.T @ keysu + query2q.T @ tagsu
    ta = np.max(a, axis=1, keepdims=True)
    e1 = np.exp(pick8(a, idx, 16) - ta)
    f1 = np.zeros((Q, T))
    f1[np.arange(Q)[:, None], idx2[np.arange(Q) % 128 // 16]] = e1
    cc = a + f1 * 4.0
    s1 = sigmoid(pick8(cc, idx3, 16) * f64(slope) + f64(thr))
    f2 = np.zeros((Q, T))
    f2[np.arange(Q)[:, None], idx2[np.arange(Q) % 128 // 16]] = s1
    dd = cc + f2
    y = pick8(dd, idx4, 16)
    return y

@@ -1,0 +1,169 @@
+from contextlib import ExitStack
+
+import concourse.mybir as mybir
+
+F32 = mybir.dt.float32
+BF16 = mybir.dt.bfloat16
+U32 = mybir.dt.uint32
+I32 = mybir.dt.int32
+U16 = mybir.dt.uint16
+U8 = mybir.dt.uint8
+FP8X4 = mybir.dt.float8_e4m3fn_x4
+FP4X4 = mybir.dt.float4_e2m1fn_x4
+ALU = mybir.AluOpType
+ACT = mybir.ActivationFunctionType
+
+D, T, I, Q = 512, 1024, 512, 128
+P = 128
+PACK = 4
+BANK = 512
+PIECE = 256
+PER_COL = 16
+KEYS_ROW = 4
+
+FLOPS = 2 * 2 * D * T * Q
+
+
+def tile_attend_echoed_parts_kernel(tc, query, query2, keys_words, keys_scales, tags_words, tags_scales,
+                                     thr, slope, offs, offs2, offs3, offs4, out):
+    nc = tc.nc
+    with ExitStack() as ctx:
+        lists = ctx.enter_context(tc.tile_pool(name="lists", bufs=1))
+        keep = ctx.enter_context(tc.tile_pool(name="keep", bufs=1))
+        psum = ctx.enter_context(tc.psum_pool(name="psum", bufs=1))
+
+        tags_plane = keep.tile([P, T], U8, name="tags_plane", align_bytes=64)
+        keys_plane = keep.tile([P, T], U8, name="keys_plane", align_bytes=64)
+        placed = keep.tile([P, T], F32, name="placed")
+
+        def load_query(src, name, queue):
+            raw = keep.tile([P, PACK, Q], F32, name=name + "_raw")
+            queue.dma_start(out=raw[:], in_=src.rearrange("(p j) q -> p j q", j=PACK))
+            return raw
+
+        def load_scales(plane, src, first_row, quadrant, queue):
+            row = 32 * quadrant + first_row
+            queue.dma_start(out=plane[row:row + 4, :].bitcast(I32),
+                            in_=src[0, 4 * quadrant:4 * quadrant + 4, :].bitcast(I32))
+
+        def load_keys(h, n, queue):
+            words = keep.tile([P, n], U32, name="keys%d" % h, align_bytes=64)
+            flat = keys_words[0].rearrange("p n t -> p (n t)")
+            queue.dma_start(out=words[:].bitcast(I32), in_=flat[:, 4 * h:4 * (h + n)].bitcast(I32))
+            return words
+
+        def load_tags(h, n, queue):
+            words = keep.tile([P, 2 * n], U8, name="tags%d" % h, align_bytes=64)
+            queue.dma_start(out=words[:].bitcast(I32), in_=tags_words[0][:, 2 * h:2 * (h + n)].bitcast(I32))
+            return words
+
+        def load_list(src, name):
+            held = lists.tile([P, I // PER_COL], U16, name=name)
+            nc.sync.dma_start(held[:], src)
+            return held
+
+        def load_column(src, name, queue):
+            held = keep.tile([P, 1], F32, name=name)
+            queue.dma_start(out=held[:], in_=src)
+            return held
+
+        def stage_scales(staged, src, quadrant, queue):
+            row = 32 * quadrant
+            queue.dma_start(out=staged[row:row + 4, :], in_=src[0, 4 * quadrant:4 * quadrant + 4, :].bitcast(I32))
+
+        def unstage_scales(plane, staged, quadrant):
+            row = 32 * quadrant
+            nc.vector.tensor_copy(out=plane[row:row + 4, :].bitcast(I32), in_=staged[row:row + 4, :])
+
+        def quantise(raw, name, on_vector):
+            grouped = keep.tile([P, Q, PACK], BF16, name=name + "_bf16", align_bytes=64)
+            nc.vector.tensor_copy(out=grouped[:, :on_vector, :].rearrange("p (c i) t -> p c t i", i=4),
+                                  in_=raw[:, :, :on_vector].rearrange("p t (c i) -> p c t i", i=4))
+            if on_vector < Q:
+                nc.scalar.activation(grouped[:, on_vector:, :].rearrange("p (c i) t -> p c t i", i=4),
+                                     raw[:, :, on_vector:].rearrange("p t (c i) -> p c t i", i=4), ACT.Copy)
+            codes = keep.tile([P, Q], U32, name=name + "_codes", align_bytes=64)
+            scales = keep.tile([P, Q], U8, name=name + "_scales", align_bytes=64)
+            nc.vector.quantize_mx(out=codes[:].bitcast(FP8X4), scales=scales[:],
+                                  in_=grouped[:].rearrange("p q t -> p (q t)"))
+            return codes, scales
+
+        nc.vector.memset(tags_plane[:].bitcast(U32), 0)
+        nc.vector.memset(keys_plane[:].bitcast(U32), 0)
+        staged = keep.tile([P, T // 4], I32, name="staged")
+        for quadrant in range(4):
+            stage_scales(staged, tags_scales, quadrant, nc.scalar if quadrant % 2 else nc.sync)
+        q2_raw = load_query(query2, "q2", nc.sync)
+        tags = load_tags(0, T, nc.sync)
+        q_raw = load_query(query, "q", nc.sync)
+        keys0 = load_keys(0, BANK, nc.sync)
+        for quadrant in range(4):
+            load_scales(keys_plane, keys_scales, KEYS_ROW, quadrant, nc.sync)
+        keys1 = load_keys(BANK, BANK, nc.sync)
+        idx = load_list(offs, "idx")
+        idx2 = load_list(offs2, "idx2")
+        idx3 = load_list(offs3, "idx3")
+        idx4 = load_list(offs4, "idx4")
+        thr_col = load_column(thr, "thr_col", nc.gpsimd)
+        slope_col = load_column(slope, "slope_col", nc.gpsimd)
+        nc.vector.memset(placed[:], 0.0)
+        for quadrant in range(4):
+            unstage_scales(tags_plane, staged, quadrant)
+
+        q2_codes, q2_scales = quantise(q2_raw, "q2", Q)
+        q_codes, q_scales = quantise(q_raw, "q", 96)
+
+        a = keep.tile([P, T], F32, name="a")
+        tops = keep.tile([P, 2], F32, name="tops")
+        neg_top = keep.tile([P, 1], F32, name="neg_top")
+        banks = [psum.tile([P, BANK], F32, name="bank%d" % h) for h in range(2)]
+
+        def keys_pass(h, words, start, stop):
+            nc.tensor.matmul_mx(out=banks[h][:], lhsT=q_codes[:].bitcast(FP8X4), lhsT_scale=q_scales[:],
+                                rhs=words.bitcast(FP8X4), rhs_scale=keys_plane[KEYS_ROW:, h * BANK:(h + 1) * BANK],
+                                start=start, stop=stop)
+
+        def tags_pass(h, words, start, stop):
+            nc.tensor.matmul_mx(out=banks[h][:], lhsT=q2_codes[:].bitcast(FP8X4), lhsT_scale=q2_scales[:],
+                                rhs=words.bitcast(FP4X4), rhs_scale=tags_plane[:, h * BANK:(h + 1) * BANK],
+                                start=start, stop=stop)
+
+        def empty_bank(h):
+            nc.vector.tensor_scalar(a[:, h * BANK:(h + 1) * BANK], banks[h][:], 1.0, None, ALU.mult, ALU.max,
+                                    accum_out=tops[:, h:h + 1])
+
+        tags_pass(0, tags[:, 0:2 * BANK], True, False)
+        tags_pass(1, tags[:, 2 * BANK:], True, False)
+        keys_pass(0, keys0[:], False, True)
+        keys_pass(1, keys1[:], False, True)
+        empty_bank(0)
+        empty_bank(1)
+
+        nc.vector.tensor_reduce(out=neg_top[:], in_=tops[:], axis=mybir.AxisListType.X, op=ALU.max, negate=True)
+
+        pieces = [(slice(s, s + PIECE), slice(s // PER_COL, (s + PIECE) // PER_COL)) for s in range(0, I, PIECE)]
+
+        e1 = keep.tile([P, I], F32, name="e1")
+        for slots, cols in pieces:
+            nc.scalar.activation(e1[:, slots], a[:].indirect(idx[:, cols]), ACT.Exp, bias=neg_top[:])
+        for slots, cols in pieces:
+            nc.vector.tensor_copy(placed[:].indirect(idx2[:, cols]), e1[:, slots])
+        cc = keep.tile([P, T], F32, name="cc")
+        nc.vector.scalar_tensor_tensor(cc[:], placed[:], 4.0, a[:], ALU.mult, ALU.add)
+
+        s1 = keep.tile([P, I], F32, name="s1")
+        for slots, cols in pieces:
+            nc.scalar.activation(s1[:, slots], cc[:].indirect(idx3[:, cols]), ACT.Sigmoid,
+                                 bias=thr_col[:], scale=slope_col[:])
+        for slots, cols in pieces:
+            nc.vector.tensor_copy(placed[:].indirect(idx2[:, cols]), s1[:, slots])
+        dd = keep.tile([P, T], F32, name="dd")
+        nc.vector.tensor_tensor(dd[:], cc[:], placed[:], ALU.add)
+
+        (slots_v, cols_v), (slots_s, cols_s) = pieces
+        y_v = keep.tile([P, PIECE], F32, name="y_v")
+        y_s = keep.tile([P, PIECE], F32, name="y_s")
+        nc.vector.tensor_copy(y_v[:], dd[:].indirect(idx4[:, cols_v]))
+        nc.scalar.activation(y_s[:], dd[:].indirect(idx4[:, cols_s]), ACT.Copy)
+        nc.sync.dma_start(out=out[:, slots_v], in_=y_v[:])
+        nc.scalar.dma_start(out=out[:, slots_s], in_=y_s[:])

@@ -90,73 +90,70 @@ def tile_attend_echoed_parts_kernel(tc, query, query2, keys_words, keys_scales, 
 
         nc.vector.memset(tags_plane[:].bitcast(U32), 0)
         nc.vector.memset(keys_plane[:].bitcast(U32), 0)
-        staged = keep.tile([P, T // 4], I32, name="staged")
-        for quadrant in range(4):
-            stage_scales(staged, tags_scales, quadrant, nc.scalar if quadrant % 2 else nc.sync)
         q2_raw = load_query(query2, "q2", nc.sync)
+        for quadrant in range(4):
+            load_scales(tags_plane, tags_scales, 0, quadrant, nc.scalar if quadrant < 2 else nc.sync)
         tags = load_tags(0, T, nc.sync)
         q_raw = load_query(query, "q", nc.sync)
-        keys0 = load_keys(0, BANK, nc.sync)
+        keys = [load_keys(0, BANK, nc.sync)]
         for quadrant in range(4):
             load_scales(keys_plane, keys_scales, KEYS_ROW, quadrant, nc.sync)
-        keys1 = load_keys(BANK, BANK, nc.sync)
+        keys.append(load_keys(BANK, BANK, nc.sync))
         idx = load_list(offs, "idx")
         idx2 = load_list(offs2, "idx2")
         idx3 = load_list(offs3, "idx3")
+        thr_col = load_column(thr, "thr_col", nc.sync)
+        slope_col = load_column(slope, "slope_col", nc.sync)
         idx4 = load_list(offs4, "idx4")
-        thr_col = load_column(thr, "thr_col", nc.gpsimd)
-        slope_col = load_column(slope, "slope_col", nc.gpsimd)
         nc.vector.memset(placed[:], 0.0)
-        for quadrant in range(4):
-            unstage_scales(tags_plane, staged, quadrant)
 
         q2_codes, q2_scales = quantise(q2_raw, "q2", Q)
         q_codes, q_scales = quantise(q_raw, "q", 96)
 
         a = keep.tile([P, T], F32, name="a")
-        tops = keep.tile([P, 2], F32, name="tops")
+        tops = keep.tile([P, T // 256], F32, name="tops")
         neg_top = keep.tile([P, 1], F32, name="neg_top")
-        banks = [psum.tile([P, BANK], F32, name="bank%d" % h) for h in range(2)]
+        GROUP = 256
+        banks = [psum.tile([P, GROUP], F32, name="bank%d" % h) for h in range(T // GROUP)]
 
         def keys_pass(h, words, start, stop):
             nc.tensor.matmul_mx(out=banks[h][:], lhsT=q_codes[:].bitcast(FP8X4), lhsT_scale=q_scales[:],
-                                rhs=words.bitcast(FP8X4), rhs_scale=keys_plane[KEYS_ROW:, h * BANK:(h + 1) * BANK],
+                                rhs=words.bitcast(FP8X4), rhs_scale=keys_plane[KEYS_ROW:, h * GROUP:(h + 1) * GROUP],
                                 start=start, stop=stop)
 
         def tags_pass(h, words, start, stop):
             nc.tensor.matmul_mx(out=banks[h][:], lhsT=q2_codes[:].bitcast(FP8X4), lhsT_scale=q2_scales[:],
-                                rhs=words.bitcast(FP4X4), rhs_scale=tags_plane[:, h * BANK:(h + 1) * BANK],
+                                rhs=words.bitcast(FP4X4), rhs_scale=tags_plane[:, h * GROUP:(h + 1) * GROUP],
                                 start=start, stop=stop)
 
         def empty_bank(h):
-            nc.vector.tensor_scalar(a[:, h * BANK:(h + 1) * BANK], banks[h][:], 1.0, None, ALU.mult, ALU.max,
+            nc.vector.tensor_scalar(a[:, h * GROUP:(h + 1) * GROUP], banks[h][:], 1.0, None, ALU.mult, ALU.max,
                                     accum_out=tops[:, h:h + 1])
 
-        tags_pass(0, tags[:, 0:2 * BANK], True, False)
-        tags_pass(1, tags[:, 2 * BANK:], True, False)
-        keys_pass(0, keys0[:], False, True)
-        keys_pass(1, keys1[:], False, True)
-        empty_bank(0)
-        empty_bank(1)
+        for h in range(4):
+            tags_pass(h, tags[:, 2 * GROUP * h:2 * GROUP * (h + 1)], True, False)
+        for h in range(4):
+            keys_pass(h, keys[h // 2][:, GROUP * (h % 2):GROUP * (h % 2 + 1)], False, True)
+            empty_bank(h)
 
         nc.vector.tensor_reduce(out=neg_top[:], in_=tops[:], axis=mybir.AxisListType.X, op=ALU.max, negate=True)
 
         pieces = [(slice(s, s + PIECE), slice(s // PER_COL, (s + PIECE) // PER_COL)) for s in range(0, I, PIECE)]
 
-        e1 = keep.tile([P, I], F32, name="e1")
-        for slots, cols in pieces:
-            nc.scalar.activation(e1[:, slots], a[:].indirect(idx[:, cols]), ACT.Exp, bias=neg_top[:])
-        for slots, cols in pieces:
-            nc.vector.tensor_copy(placed[:].indirect(idx2[:, cols]), e1[:, slots])
+        e1 = [keep.tile([P, PIECE], F32, name="e1_%d" % n) for n in range(len(pieces))]
+        for part, (slots, cols) in zip(e1, pieces):
+            nc.scalar.activation(part[:], a[:].indirect(idx[:, cols]), ACT.Exp, bias=neg_top[:])
+        for part, (slots, cols) in zip(e1, pieces):
+            nc.vector.tensor_copy(placed[:].indirect(idx2[:, cols]), part[:])
         cc = keep.tile([P, T], F32, name="cc")
         nc.vector.scalar_tensor_tensor(cc[:], placed[:], 4.0, a[:], ALU.mult, ALU.add)
 
-        s1 = keep.tile([P, I], F32, name="s1")
-        for slots, cols in pieces:
-            nc.scalar.activation(s1[:, slots], cc[:].indirect(idx3[:, cols]), ACT.Sigmoid,
+        s1 = [keep.tile([P, PIECE], F32, name="s1_%d" % n) for n in range(len(pieces))]
+        for part, (slots, cols) in zip(s1, pieces):
+            nc.scalar.activation(part[:], cc[:].indirect(idx3[:, cols]), ACT.Sigmoid,
                                  bias=thr_col[:], scale=slope_col[:])
-        for slots, cols in pieces:
-            nc.vector.tensor_copy(placed[:].indirect(idx2[:, cols]), s1[:, slots])
+        for part, (slots, cols) in zip(s1, pieces):
+            nc.vector.tensor_copy(placed[:].indirect(idx2[:, cols]), part[:])
         dd = keep.tile([P, T], F32, name="dd")
         nc.vector.tensor_tensor(dd[:], cc[:], placed[:], ALU.add)
 

from contextlib import ExitStack

import concourse.mybir as mybir

F32 = mybir.dt.float32
BF16 = mybir.dt.bfloat16
U32 = mybir.dt.uint32
I32 = mybir.dt.int32
U16 = mybir.dt.uint16
U8 = mybir.dt.uint8
FP8X4 = mybir.dt.float8_e4m3fn_x4
FP4X4 = mybir.dt.float4_e2m1fn_x4
ALU = mybir.AluOpType
ACT = mybir.ActivationFunctionType

D, T, I, Q = 512, 1024, 512, 128
P = 128
PACK = 4
BANK = 512
PIECE = 256
PER_COL = 16
KEYS_ROW = 4

FLOPS = 2 * 2 * D * T * Q


def tile_attend_echoed_parts_kernel(tc, query, query2, keys_words, keys_scales, tags_words, tags_scales,
                                     thr, slope, offs, offs2, offs3, offs4, out):
    nc = tc.nc
    with ExitStack() as ctx:
        lists = ctx.enter_context(tc.tile_pool(name="lists", bufs=1))
        keep = ctx.enter_context(tc.tile_pool(name="keep", bufs=1))
        psum = ctx.enter_context(tc.psum_pool(name="psum", bufs=1))

        tags_plane = keep.tile([P, T], U8, name="tags_plane", align_bytes=64)
        keys_plane = keep.tile([P, T], U8, name="keys_plane", align_bytes=64)
        placed = keep.tile([P, T], F32, name="placed")

        def load_query(src, name, queue):
            raw = keep.tile([P, PACK, Q], F32, name=name + "_raw")
            queue.dma_start(out=raw[:], in_=src.rearrange("(p j) q -> p j q", j=PACK))
            return raw

        def load_scales(plane, src, first_row, quadrant, queue):
            row = 32 * quadrant + first_row
            queue.dma_start(out=plane[row:row + 4, :].bitcast(I32),
                            in_=src[0, 4 * quadrant:4 * quadrant + 4, :].bitcast(I32))

        def load_keys(h, n, queue):
            words = keep.tile([P, n], U32, name="keys%d" % h, align_bytes=64)
            flat = keys_words[0].rearrange("p n t -> p (n t)")
            queue.dma_start(out=words[:].bitcast(I32), in_=flat[:, 4 * h:4 * (h + n)].bitcast(I32))
            return words

        def load_tags(h, n, queue):
            words = keep.tile([P, 2 * n], U8, name="tags%d" % h, align_bytes=64)
            queue.dma_start(out=words[:].bitcast(I32), in_=tags_words[0][:, 2 * h:2 * (h + n)].bitcast(I32))
            return words

        def load_list(src, name):
            held = lists.tile([P, I // PER_COL], U16, name=name)
            nc.sync.dma_start(held[:], src)
            return held

        def load_column(src, name, queue):
            held = keep.tile([P, 1], F32, name=name)
            queue.dma_start(out=held[:], in_=src)
            return held

        def stage_scales(staged, src, quadrant, queue):
            row = 32 * quadrant
            queue.dma_start(out=staged[row:row + 4, :], in_=src[0, 4 * quadrant:4 * quadrant + 4, :].bitcast(I32))

        def unstage_scales(plane, staged, quadrant):
            row = 32 * quadrant
            nc.vector.tensor_copy(out=plane[row:row + 4, :].bitcast(I32), in_=staged[row:row + 4, :])

        def quantise(raw, name, on_vector):
            grouped = keep.tile([P, Q, PACK], BF16, name=name + "_bf16", align_bytes=64)
            nc.vector.tensor_copy(out=grouped[:, :on_vector, :].rearrange("p (c i) t -> p c t i", i=4),
                                  in_=raw[:, :, :on_vector].rearrange("p t (c i) -> p c t i", i=4))
            if on_vector < Q:
                nc.scalar.activation(grouped[:, on_vector:, :].rearrange("p (c i) t -> p c t i", i=4),
                                     raw[:, :, on_vector:].rearrange("p t (c i) -> p c t i", i=4), ACT.Copy)
            codes = keep.tile([P, Q], U32, name=name + "_codes", align_bytes=64)
            scales = keep.tile([P, Q], U8, name=name + "_scales", align_bytes=64)
            nc.vector.quantize_mx(out=codes[:].bitcast(FP8X4), scales=scales[:],
                                  in_=grouped[:].rearrange("p q t -> p (q t)"))
            return codes, scales

        nc.vector.memset(tags_plane[:].bitcast(U32), 0)
        nc.vector.memset(keys_plane[:].bitcast(U32), 0)
        q2_raw = load_query(query2, "q2", nc.sync)
        for quadrant in range(4):
            load_scales(tags_plane, tags_scales, 0, quadrant, nc.scalar if quadrant < 2 else nc.sync)
        tags = load_tags(0, T, nc.sync)
        q_raw = load_query(query, "q", nc.sync)
        keys = [load_keys(0, BANK, nc.sync)]
        for quadrant in range(4):
            load_scales(keys_plane, keys_scales, KEYS_ROW, quadrant, nc.sync)
        keys.append(load_keys(BANK, BANK, nc.sync))
        idx = load_list(offs, "idx")
        idx2 = load_list(offs2, "idx2")
        idx3 = load_list(offs3, "idx3")
        thr_col = load_column(thr, "thr_col", nc.sync)
        slope_col = load_column(slope, "slope_col", nc.sync)
        idx4 = load_list(offs4, "idx4")
        nc.vector.memset(placed[:], 0.0)

        q2_codes, q2_scales = quantise(q2_raw, "q2", Q)
        q_codes, q_scales = quantise(q_raw, "q", 96)

        a = keep.tile([P, T], F32, name="a")
        tops = keep.tile([P, T // 256], F32, name="tops")
        neg_top = keep.tile([P, 1], F32, name="neg_top")
        GROUP = 256
        banks = [psum.tile([P, GROUP], F32, name="bank%d" % h) for h in range(T // GROUP)]

        def keys_pass(h, words, start, stop):
            nc.tensor.matmul_mx(out=banks[h][:], lhsT=q_codes[:].bitcast(FP8X4), lhsT_scale=q_scales[:],
                                rhs=words.bitcast(FP8X4), rhs_scale=keys_plane[KEYS_ROW:, h * GROUP:(h + 1) * GROUP],
                                start=start, stop=stop)

        def tags_pass(h, words, start, stop):
            nc.tensor.matmul_mx(out=banks[h][:], lhsT=q2_codes[:].bitcast(FP8X4), lhsT_scale=q2_scales[:],
                                rhs=words.bitcast(FP4X4), rhs_scale=tags_plane[:, h * GROUP:(h + 1) * GROUP],
                                start=start, stop=stop)

        def empty_bank(h):
            nc.vector.tensor_scalar(a[:, h * GROUP:(h + 1) * GROUP], banks[h][:], 1.0, None, ALU.mult, ALU.max,
                                    accum_out=tops[:, h:h + 1])

        for h in range(4):
            tags_pass(h, tags[:, 2 * GROUP * h:2 * GROUP * (h + 1)], True, False)
        for h in range(4):
            keys_pass(h, keys[h // 2][:, GROUP * (h % 2):GROUP * (h % 2 + 1)], False, True)
            empty_bank(h)

        nc.vector.tensor_reduce(out=neg_top[:], in_=tops[:], axis=mybir.AxisListType.X, op=ALU.max, negate=True)

        pieces = [(slice(s, s + PIECE), slice(s // PER_COL, (s + PIECE) // PER_COL)) for s in range(0, I, PIECE)]

        e1 = [keep.tile([P, PIECE], F32, name="e1_%d" % n) for n in range(len(pieces))]
        for part, (slots, cols) in zip(e1, pieces):
            nc.scalar.activation(part[:], a[:].indirect(idx[:, cols]), ACT.Exp, bias=neg_top[:])
        for part, (slots, cols) in zip(e1, pieces):
            nc.vector.tensor_copy(placed[:].indirect(idx2[:, cols]), part[:])
        cc = keep.tile([P, T], F32, name="cc")
        nc.vector.scalar_tensor_tensor(cc[:], placed[:], 4.0, a[:], ALU.mult, ALU.add)

        s1 = [keep.tile([P, PIECE], F32, name="s1_%d" % n) for n in range(len(pieces))]
        for part, (slots, cols) in zip(s1, pieces):
            nc.scalar.activation(part[:], cc[:].indirect(idx3[:, cols]), ACT.Sigmoid,
                                 bias=thr_col[:], scale=slope_col[:])
        for part, (slots, cols) in zip(s1, pieces):
            nc.vector.tensor_copy(placed[:].indirect(idx2[:, cols]), part[:])
        dd = keep.tile([P, T], F32, name="dd")
        nc.vector.tensor_tensor(dd[:], cc[:], placed[:], ALU.add)

        (slots_v, cols_v), (slots_s, cols_s) = pieces
        y_v = keep.tile([P, PIECE], F32, name="y_v")
        y_s = keep.tile([P, PIECE], F32, name="y_s")
        nc.vector.tensor_copy(y_v[:], dd[:].indirect(idx4[:, cols_v]))
        nc.scalar.activation(y_s[:], dd[:].indirect(idx4[:, cols_s]), ACT.Copy)
        nc.sync.dma_start(out=out[:, slots_v], in_=y_v[:])
        nc.scalar.dma_start(out=out[:, slots_s], in_=y_s[:])
